import numpy as np
import ml_dtypes


def mxq(x, axis, fmt="e4m3"):
    dtype, down = {"e4m3": (ml_dtypes.float8_e4m3fn, 7), "e5m2": (ml_dtypes.float8_e5m2, 14)}[fmt]
    v = np.moveaxis(np.asarray(x, np.float32).astype(ml_dtypes.bfloat16).astype(np.float64), axis, -1)
    blocks = v.reshape(v.shape[:-1] + (-1, 32))
    amax = np.abs(blocks).max(-1, keepdims=True)
    byte = np.maximum(np.where(amax > 0, np.frexp(amax)[1] - 1 + 127, 0) - down, 1)
    scale = np.exp2(byte - 127.0)
    codes = (blocks / scale).astype(np.float32).astype(dtype).astype(np.float64)
    return np.moveaxis((codes * scale).reshape(v.shape), -1, axis)


WIDE = False


def mx_kscale(k):
    if not WIDE:
        return np.ones(k)
    levels = np.array([10, -10, 5, -5, 0])
    if k % 512:
        return np.exp2(np.random.permutation(np.resize(levels, k // 32))).repeat(32)
    a = np.empty((k // 512, 16))
    for p in range(k // 512):
        a[p, :8] = np.random.permutation(np.resize(levels, 8))
        for g in range(8):
            far = levels[np.abs(levels - a[p, g]) >= 10]
            a[p, g + 8] = far[np.random.randint(len(far))]
    return np.exp2(a.ravel()).repeat(32)


def f64(x):
    return np.asarray(x).astype(np.float64)


def striped(idx):
    return np.tile(idx.reshape(-1, 16).T, (8, 1)).astype(np.uint16)


def unstriped(offs):
    return offs[:16].T.reshape(-1).astype(np.int64)


def striped8(idx):
    return np.concatenate([x.reshape(-1, 16).T for x in idx]).astype(np.uint16)


def runs(offs, k):
    lists = np.stack([offs[16 * r : 16 * r + 16].T.reshape(-1) for r in range(8)]).astype(np.int64)
    return lists[np.arange(k) % 512 // 64]


def pack_weight(w):
    k, n = w.shape
    w = f64(np.asarray(w, np.float32).astype(ml_dtypes.bfloat16)).reshape(k // 32, 32, n)
    amax = np.abs(w).max(1)
    byte = np.clip(np.where(amax > 0, np.frexp(amax)[1] - 1 + 127 - 7, 1), 1, 254)
    scaled = (w * np.exp2(127.0 - byte)[:, None, :]).reshape(k, n).astype(np.float32)
    words = np.ascontiguousarray(scaled.reshape(k // 512, 128, 4, n).transpose(0, 1, 3, 2)).astype(ml_dtypes.float8_e4m3fn).view(np.uint8)
    return words, np.ascontiguousarray(byte.astype(np.uint8).reshape(k // 512, 16, n))


def unpack_weight(words, scales):
    g, p, n, _ = words.shape
    vals = np.ascontiguousarray(words).view(ml_dtypes.float8_e4m3fn).astype(np.float64) * np.repeat(np.exp2(scales.astype(np.float64) - 127.0), 8, axis=1)[..., None]
    return vals.transpose(0, 1, 3, 2).reshape(g * 512, n)

def planes(y):
    n, m = y.shape
    v = y.astype(np.float32).astype(ml_dtypes.bfloat16).astype(np.float64).reshape(n // 32, 32, m)
    top = np.abs(v).max(1)
    byte = np.clip(np.where(top > 0, np.frexp(top)[1] - 1 + 127 - 7, 1), 1, 254)
    codes = (v * np.exp2(127.0 - byte)[:, None, :]).reshape(n, m).astype(np.float32).astype(ml_dtypes.float8_e4m3fn).view(np.uint8)
    words = codes.reshape(n // 512, 128, 4, m).transpose(0, 1, 3, 2)
    return np.ascontiguousarray(words), np.ascontiguousarray(byte.astype(np.uint8).reshape(n // 512, 16, m))


K, T, S, H, W = 512, 2048, 512, 512, 256


def setup_inputs():
    n = np.random.standard_normal
    s = mx_kscale(K)[:, None]
    u = mx_kscale(S)
    packed_xT = pack_weight(n((K, T)) * s)
    return {
        "x_words": packed_xT[0],
        "x_scales": packed_xT[1],
        "wa": (n((K, H)) / np.sqrt(K) / s).astype(np.float32),
        "wb": (n((K, H)) / np.sqrt(K) / s).astype(np.float32),
        "gt": (np.random.uniform(0.5, 1.5, (S, 1)) * u[:, None]).astype(np.float32),
        "gi": (np.random.uniform(0.5, 1.5, (S, 1)) / u[:, None]).astype(np.float32),
        "offs": striped(np.random.permutation(T)[:S]),
        "two": striped(np.random.permutation(T)[:S]),
        "n1": striped(np.random.permutation(H)[:W]),
        "n2": striped(np.random.permutation(H)[:W]),
        "n3": striped8(np.stack([np.random.permutation(H) for _ in range(8)])),
        "n4": striped8(np.stack([np.random.permutation(H) for _ in range(8)])),
    }


def reference(x_words, x_scales, wa, wb, gt, gi, offs, two, n1, n2, n3, n4):
    x_two = unpack_weight(x_words, x_scales)[:, unstriped(two)]
    b = x_two.T @ mxq(f64(wb), 0, "e4m3")
    xq = unpack_weight(x_words, x_scales)[:, unstriped(offs)]
    a = xq.T @ mxq(f64(wa), 0, "e4m3")
    ra = b[:, unstriped(n2)] - (0.5 * a[:, unstriped(n1)])
    ds = a.copy()
    ds[:, unstriped(n1)] = ra
    z = f64(gt) * ds
    z2 = f64(gi) * b
    cv = 0.0625 * ((mxq(z, 0, "e4m3").T @ mxq(z2, 0, "e4m3")))
    out_0 = (cv[np.arange(H)[:, None], runs(n3, H)]) / (np.abs(cv) + np.abs(cv[np.arange(H)[:, None], runs(n4, H)]) + 0.5)
    return (out_0,) + planes(out_0)

@@ -1,0 +1,276 @@
+from contextlib import ExitStack
+
+import concourse.mybir as mybir
+
+F32 = mybir.dt.float32
+BF16 = mybir.dt.bfloat16
+I32 = mybir.dt.int32
+U32 = mybir.dt.uint32
+U16 = mybir.dt.uint16
+U8 = mybir.dt.uint8
+FP8X4 = mybir.dt.float8_e4m3fn_x4
+ALU = mybir.AluOpType
+ACT = mybir.ActivationFunctionType
+
+P = 128
+PACK = 4
+K, T, S, H, W = 512, 2048, 512, 512, 256
+HALF = 256
+FLOPS = 3 * 2 * 512 * 512 * 512
+
+
+def interleave_views(dst, src):
+    return dst.rearrange("p (c i) j -> p c j i", i=4), src.rearrange("p j (c i) -> p c j i", i=4)
+
+
+def tile_picked_momtputbnorm2_none_po_kernel(tc, x_words, x_scales, wa, wb, gt, gi, offs, two, n1, n2, n3, n4, out_0, out_1, out_2):
+    nc = tc.nc
+    with ExitStack() as ctx:
+        lists = ctx.enter_context(tc.tile_pool(name="lists", bufs=1))
+        sb = ctx.enter_context(tc.tile_pool(name="sb", bufs=1))
+        psum = ctx.enter_context(tc.psum_pool(name="psum", bufs=1))
+
+        def tile(shape, dtype, name, tag=None):
+            return sb.tile(shape, dtype, name=name, tag=tag or name, align_bytes=64)
+
+        def load_list(src, name):
+            held = lists.tile([P, src.shape[1]], U16, name=name)
+            nc.sync.dma_start(held[:], src)
+            return held
+
+        def mx_tile(name, width):
+            return tile([P, width], U32, name + "_codes"), tile([P, width], U8, name + "_scales")
+
+        def quantize(operand, cols, grouped):
+            codes, scales = operand
+            nc.vector.quantize_mx(out=codes[:, cols].bitcast(FP8X4), scales=scales[:, cols],
+                                  in_=grouped.rearrange("p n j -> p (n j)"))
+
+        def product(bank, stationary, t, moving, cols):
+            rows = slice(t * P, (t + 1) * P)
+            nc.tensor.matmul_mx(out=bank[:, cols], lhsT=stationary[0][:, rows].bitcast(FP8X4), lhsT_scale=stationary[1][:, rows],
+                                rhs=moving[0][:, cols].bitcast(FP8X4), rhs_scale=moving[1][:, cols], start=True, stop=True)
+
+        halves = [slice(h * HALF, (h + 1) * HALF) for h in range(2)]
+        whole = slice(0, H)
+
+        xs = tile([P, T], U8, "xs")
+        nc.gpsimd.memset(xs[:].bitcast(I32), 0)
+        for q in range(4):
+            nc.scalar.dma_start(xs[32 * q : 32 * q + 4, :].bitcast(I32), x_scales[0, 4 * q : 4 * q + 4, :].bitcast(I32))
+
+        def load_weight_half(w, h, name):
+            raw = tile([P, PACK, HALF], F32, name)
+            nc.sync.dma_start(raw[:], w.rearrange("(p j) n -> p j n", j=PACK)[:, :, halves[h]])
+            return raw
+
+        two_t = load_list(two, "two_t")
+        offs_t = load_list(offs, "offs_t")
+        wb_raw = [load_weight_half(wb, h, "wb_raw%d" % h) for h in range(2)]
+        xw = tile([P, T], I32, "xw")
+        nc.sync.dma_start(xw[:], x_words[0].rearrange("p n r -> p (n r)").bitcast(I32))
+        wa_raw = [load_weight_half(wa, h, "wa_raw%d" % h) for h in range(2)]
+        n2_t = load_list(n2, "n2_t")
+        n1_t = load_list(n1, "n1_t")
+        gi_t = tile([P, PACK], F32, "gi_t")
+        nc.sync.dma_start(gi_t[:], gi.rearrange("(p t) o -> p (t o)", t=PACK))
+        gt_t = tile([P, PACK], F32, "gt_t")
+        nc.sync.dma_start(gt_t[:], gt.rearrange("(p t) o -> p (t o)", t=PACK))
+        n4_t = load_list(n4, "n4_t")
+        n3_t = load_list(n3, "n3_t")
+
+        def pick_scales(lst, name):
+            picked = tile([P, S], U8, name + "_picked")
+            nc.vector.tensor_copy(picked[:], xs[:].indirect(lst[:]))
+            dealt = tile([P, S], U8, name + "_dealt")
+            nc.vector.tensor_copy(dealt[:].rearrange("p (t m) -> p m t", t=PACK), picked[:].rearrange("p (m t) -> p m t", t=PACK))
+            return dealt
+
+        def pick_words(lst, name):
+            dealt = tile([P, S], U32, name)
+            nc.vector.tensor_copy(dealt[:].rearrange("p (t m) -> p m t", t=PACK), xw[:].bitcast(U32).indirect(lst[:]))
+            return dealt
+
+        def group_weight(raw, name, copy):
+            grouped = tile([P, HALF, PACK], BF16, name)
+            dst, src = interleave_views(grouped[:], raw[:])
+            copy(dst, src)
+            return grouped
+
+        wbq = mx_tile("wbq", H)
+        waq = mx_tile("waq", H)
+        wb_grouped = [group_weight(wb_raw[h], "wb_grouped%d" % h, nc.scalar.copy) for h in range(2)]
+        xb_scales = pick_scales(two_t, "xb_scales")
+        xa_scales = pick_scales(offs_t, "xa_scales")
+        for h in range(2):
+            quantize(wbq, halves[h], wb_grouped[h][:])
+        xb = (pick_words(two_t, "xb_words"), xb_scales)
+        xa = (pick_words(offs_t, "xa_words"), xa_scales)
+        b_bank = [psum.tile([P, H], F32, name="b_bank%d" % t, tag="bank%d" % t) for t in range(PACK)]
+        for t in range(PACK):
+            product(b_bank[t], xb, t, wbq, whole)
+        wa_grouped = [group_weight(wa_raw[0], "wa_grouped0", nc.scalar.copy), group_weight(wa_raw[1], "wa_grouped1", nc.vector.tensor_copy)]
+        a_bank = [psum.tile([P, H], F32, name="a_bank%d" % t, tag="bank%d" % (PACK + t)) for t in range(PACK)]
+        for h in range(2):
+            quantize(waq, halves[h], wa_grouped[h][:])
+            for t in range(PACK):
+                product(a_bank[t], xa, t, waq, halves[h])
+
+        ds = [tile([P, H], F32, "ds%d" % t) for t in range(PACK)]
+        ga = [tile([P, W], F32, "ga%d" % t) for t in range(PACK)]
+        gb = [tile([P, W], F32, "gb%d" % t) for t in range(PACK)]
+        ra = [tile([P, W], F32, "ra%d" % t) for t in range(PACK)]
+        b_sb = {}
+
+        def fetch_a(t):
+            nc.vector.tensor_copy(ds[t][:], a_bank[t][:])
+            nc.scalar.activation(ga[t][:], ds[t][:].indirect(n1_t[:]), ACT.Copy)
+
+        def fetch_b(t, copy, tag):
+            b_sb[t] = tile([P, H], F32, "b_sb%d" % t, tag)
+            copy(b_sb[t][:], b_bank[t][:])
+            nc.scalar.activation(gb[t][:], b_sb[t][:].indirect(n2_t[:]), ACT.Copy)
+
+        def put(t):
+            nc.vector.scalar_tensor_tensor(out=ra[t][:], in0=ga[t][:], scalar=-0.5, in1=gb[t][:], op0=ALU.mult, op1=ALU.add)
+            nc.scalar.activation(ds[t][:].indirect(n1_t[:]), ra[t][:], ACT.Copy)
+
+        def weigh_z(t):
+            nc.vector.tensor_scalar(out=z_planes[:, t, :].rearrange("p (u m) -> p m u", u=PACK),
+                                    in0=ds[t][:].rearrange("p (m u) -> p m u", u=PACK),
+                                    scalar1=gt_t[:, t : t + 1], scalar2=None, op0=ALU.mult)
+
+        def weigh_z2(t):
+            nc.vector.tensor_scalar(out=z2_planes[:, t, :], in0=b_sb[t][:], scalar1=gi_t[:, t : t + 1], scalar2=None, op0=ALU.mult)
+
+        fetch_b(0, nc.scalar.copy, "wa_raw0")
+        fetch_b(1, nc.scalar.copy, "wa_grouped0")
+        fetch_a(0)
+        fetch_a(1)
+        fetch_b(2, nc.vector.tensor_copy, "wa_grouped1")
+        put(0)
+        fetch_a(2)
+        fetch_b(3, nc.vector.tensor_copy, "ga0")
+        put(1)
+        fetch_a(3)
+        put(2)
+        put(3)
+        z2_planes = tile([P, PACK, H], BF16, "z2_planes", "ga1")
+        z_planes = tile([P, PACK - 1, H], BF16, "z_planes")
+        for t in range(PACK):
+            weigh_z2(t)
+        z2_grouped = tile([P, H, PACK], BF16, "z2_grouped")
+        dst, src = interleave_views(z2_grouped[:], z2_planes[:])
+        nc.vector.tensor_copy(dst, src)
+        z2q = mx_tile("z2q", H)
+        quantize(z2q, whole, z2_grouped[:])
+        for t in range(PACK - 1):
+            weigh_z(t)
+
+        zq = mx_tile("zq", H)
+        z_grouped = [tile([P, P, PACK], BF16, "z_grouped%d" % u) for u in range(PACK)]
+        cv_bank = [psum.tile([P, H], F32, name="cv_bank%d" % u, tag="bank%d" % u) for u in range(PACK)]
+        cv = [tile([P, H], F32, "cv%d" % u) for u in range(PACK)]
+        size = [tile([P, H], F32, "size%d" % u) for u in range(PACK)]
+
+        last = PACK - 1
+        for u in range(PACK):
+            dst, src = interleave_views(z_grouped[u][:, :, 0:last], z_planes[:, :, u * P : (u + 1) * P])
+            nc.vector.tensor_copy(dst, src)
+
+        def weigh_last(u):
+            nc.vector.tensor_scalar(out=z_grouped[u][:, :, last], in0=ds[last][:].rearrange("p (m u) -> p u m", u=PACK)[:, u, :],
+                                    scalar1=gt_t[:, last:], scalar2=None, op0=ALU.mult)
+
+        weigh_last(0)
+        for u in range(PACK):
+            if u + 1 < PACK:
+                weigh_last(u + 1)
+            quantize(zq, slice(u * P, (u + 1) * P), z_grouped[u][:])
+            product(cv_bank[u], zq, u, z2q, whole)
+
+        def empty_cv(u):
+            nc.vector.tensor_scalar(out=cv[u][:], in0=cv_bank[u][:], scalar1=0.0625, scalar2=None, op0=ALU.mult)
+
+        def size_on_scalar(u):
+            nc.scalar.activation(size[u][:], cv_bank[u][:], ACT.Abs, scale=0.0625)
+
+        def size_on_vector(u):
+            nc.vector.scalar_tensor_tensor(out=size[u][:], in0=cv_bank[u][:], scalar=-0.0625, in1=cv[u][:], op0=ALU.mult, op1=ALU.max)
+
+        out_rows = out_0.rearrange("(p u) n -> p u n", u=PACK)
+        out_words = out_1[0].rearrange("p n r -> p (n r)").bitcast(I32)
+        y_scales = tile([P, H], U8, "y_scales")
+        edges = [0, 256, 384, 512]
+        chunks = range(len(edges) - 1)
+        cols = [slice(edges[c], edges[c + 1]) for c in chunks]
+        entries = [slice(edges[c] // 16, edges[c + 1] // 16) for c in chunks]
+        width = [edges[c + 1] - edges[c] for c in chunks]
+        y = [tile([P, PACK, width[c]], F32, "y%d" % c) for c in chunks]
+        far, den, root, top = {}, {}, {}, {}
+
+        def fetch_far(c, us):
+            key = (c, us[0])
+            far[key] = tile([P, len(us), width[c]], F32, "far%d_%d" % key)
+            den[key] = tile([P, len(us), width[c]], F32, "den%d_%d" % key)
+            for i, u in enumerate(us):
+                nc.scalar.activation(far[key][:, i, :], size[u][:].indirect(n4_t[:, entries[c]]), ACT.Copy)
+                nc.vector.scalar_tensor_tensor(out=den[key][:, i, :], in0=size[u][:, cols[c]], scalar=0.5, in1=far[key][:, i, :], op0=ALU.add, op1=ALU.add)
+
+        def invert(c, us):
+            key = (c, us[0])
+            root[key] = tile([P, len(us), width[c]], F32, "root%d_%d" % key)
+            nc.scalar.activation(root[key][:], den[key][:], ACT.Abs_reciprocal_sqrt)
+            nc.vector.tensor_tensor(out=far[key][:], in0=root[key][:], in1=root[key][:], op=ALU.mult)
+
+        def fetch_top(c, us, each):
+            key = (c, us[0])
+            top[key] = tile([P, len(us), width[c]], F32, "top%d_%d" % key, "den%d_%d" % key)
+            for i, u in enumerate(us):
+                nc.scalar.activation(top[key][:, i, :], cv[u][:].indirect(n3_t[:, entries[c]]), ACT.Copy)
+                if each:
+                    nc.vector.tensor_tensor(out=y[c][:, u, :], in0=top[key][:, i, :], in1=far[key][:, i, :], op=ALU.mult)
+            if not each:
+                nc.vector.tensor_tensor(out=y[c][:, us[0] : us[-1] + 1, :], in0=top[key][:], in1=far[key][:], op=ALU.mult)
+
+        def hand_out(c):
+            nc.sync.dma_start(out_rows[:, :, cols[c]], y[c][:])
+            y_grouped = tile([P, width[c], PACK], BF16, "y_grouped%d" % c)
+            dst, src = interleave_views(y_grouped[:], y[c][:])
+            nc.vector.tensor_copy(dst, src)
+            y_codes = tile([P, width[c]], U32, "y_codes%d" % c)
+            nc.vector.quantize_mx(out=y_codes[:].bitcast(FP8X4), scales=y_scales[:, cols[c]], in_=y_grouped[:].rearrange("p n j -> p (n j)"))
+            nc.sync.dma_start(out_words[:, cols[c]], y_codes[:].bitcast(I32))
+
+        size_on_scalar(0)
+        empty_cv(0)
+        fetch_far(0, [0])
+        empty_cv(1)
+        size_on_vector(1)
+        invert(0, [0])
+        fetch_top(0, [0], True)
+        fetch_far(0, [1])
+        empty_cv(2)
+        size_on_vector(2)
+        invert(0, [1])
+        fetch_top(0, [1], True)
+        fetch_far(0, [2])
+        empty_cv(3)
+        size_on_vector(3)
+        invert(0, [2])
+        fetch_top(0, [2], True)
+        fetch_far(0, [3])
+        invert(0, [3])
+        fetch_far(1, [0, 1, 2, 3])
+        fetch_top(0, [3], True)
+        fetch_far(2, [0, 1, 2, 3])
+        invert(1, [0, 1, 2, 3])
+        hand_out(0)
+        fetch_top(1, [0, 1, 2, 3], False)
+        invert(2, [0, 1, 2, 3])
+        hand_out(1)
+        fetch_top(2, [0, 1, 2, 3], True)
+        hand_out(2)
+        for q in range(4):
+            queue = nc.scalar if q % 2 else nc.sync
+            queue.dma_start(out_2[0, 4 * q : 4 * q + 4, :].bitcast(I32), y_scales[32 * q : 32 * q + 4, :].bitcast(I32))

@@ -1,6 +1,7 @@
 from contextlib import ExitStack
 
 import concourse.mybir as mybir
+from concourse.masks import make_identity
 
 F32 = mybir.dt.float32
 BF16 = mybir.dt.bfloat16
@@ -28,9 +29,12 @@ def tile_picked_momtputbnorm2_none_po_kernel(tc, x_words, x_scales, wa, wb, gt, 
     with ExitStack() as ctx:
         lists = ctx.enter_context(tc.tile_pool(name="lists", bufs=1))
         sb = ctx.enter_context(tc.tile_pool(name="sb", bufs=1))
+        shared = ctx.enter_context(tc.tile_pool(name="shared", bufs=1))
         psum = ctx.enter_context(tc.psum_pool(name="psum", bufs=1))
 
-        def tile(shape, dtype, name, tag=None):
+        def tile(shape, dtype, name, tag=None, at=None):
+            if at is not None:
+                return shared.tile(shape, dtype, name=name, align_bytes=64, offset=at)
             return sb.tile(shape, dtype, name=name, tag=tag or name, align_bytes=64)
 
         def load_list(src, name):
@@ -55,21 +59,23 @@ def tile_picked_momtputbnorm2_none_po_kernel(tc, x_words, x_scales, wa, wb, gt, 
         whole = slice(0, H)
 
         xs = tile([P, T], U8, "xs")
-        nc.gpsimd.memset(xs[:].bitcast(I32), 0)
+        nc.vector.memset(xs[:].bitcast(I32), 0)
         for q in range(4):
             nc.scalar.dma_start(xs[32 * q : 32 * q + 4, :].bitcast(I32), x_scales[0, 4 * q : 4 * q + 4, :].bitcast(I32))
 
-        def load_weight_half(w, h, name):
-            raw = tile([P, PACK, HALF], F32, name)
+        def load_weight_half(w, h, name, at=None):
+            raw = tile([P, PACK, HALF], F32, name, at=at)
             nc.sync.dma_start(raw[:], w.rearrange("(p j) n -> p j n", j=PACK)[:, :, halves[h]])
             return raw
 
         two_t = load_list(two, "two_t")
         offs_t = load_list(offs, "offs_t")
-        wb_raw = [load_weight_half(wb, h, "wb_raw%d" % h) for h in range(2)]
+        wb_whole = tile([P, PACK, H], F32, "wb_whole")
+        nc.sync.dma_start(wb_whole[:], wb.rearrange("(p j) n -> p j n", j=PACK))
+        wa_raw = [load_weight_half(wa, 0, "wa_raw0")]
         xw = tile([P, T], I32, "xw")
         nc.sync.dma_start(xw[:], x_words[0].rearrange("p n r -> p (n r)").bitcast(I32))
-        wa_raw = [load_weight_half(wa, h, "wa_raw%d" % h) for h in range(2)]
+        wa_raw.append(load_weight_half(wa, 1, "wa_raw1", at=0))
         n2_t = load_list(n2, "n2_t")
         n1_t = load_list(n1, "n1_t")
         gi_t = tile([P, PACK], F32, "gi_t")
@@ -82,6 +88,9 @@ def tile_picked_momtputbnorm2_none_po_kernel(tc, x_words, x_scales, wa, wb, gt, 
         def pick_scales(lst, name):
             picked = tile([P, S], U8, name + "_picked")
             nc.vector.tensor_copy(picked[:], xs[:].indirect(lst[:]))
+            return picked
+
+        def deal_scales(picked, name):
             dealt = tile([P, S], U8, name + "_dealt")
             nc.vector.tensor_copy(dealt[:].rearrange("p (t m) -> p m t", t=PACK), picked[:].rearrange("p (m t) -> p m t", t=PACK))
             return dealt
@@ -99,22 +108,27 @@ def tile_picked_momtputbnorm2_none_po_kernel(tc, x_words, x_scales, wa, wb, gt, 
 
         wbq = mx_tile("wbq", H)
         waq = mx_tile("waq", H)
-        wb_grouped = [group_weight(wb_raw[h], "wb_grouped%d" % h, nc.scalar.copy) for h in range(2)]
-        xb_scales = pick_scales(two_t, "xb_scales")
-        xa_scales = pick_scales(offs_t, "xa_scales")
+        wb_grouped = tile([P, H, PACK], BF16, "wb_grouped")
+        wa_grouped = tile([P, H, PACK], BF16, "wa_grouped", at=4096)
+        dst, src = interleave_views(wb_grouped[:], wb_whole[:])
+        nc.scalar.copy(dst, src)
         for h in range(2):
-            quantize(wbq, halves[h], wb_grouped[h][:])
+            dst, src = interleave_views(wa_grouped[:, halves[h], :], wa_raw[h][:])
+            nc.scalar.copy(dst, src)
+        xb_picked = pick_scales(two_t, "xb_scales")
+        xa_picked = pick_scales(offs_t, "xa_scales")
+        xb_scales = deal_scales(xb_picked, "xb_scales")
+        xa_scales = deal_scales(xa_picked, "xa_scales")
+        quantize(wbq, whole, wb_grouped[:])
         xb = (pick_words(two_t, "xb_words"), xb_scales)
         xa = (pick_words(offs_t, "xa_words"), xa_scales)
+        quantize(waq, whole, wa_grouped[:])
         b_bank = [psum.tile([P, H], F32, name="b_bank%d" % t, tag="bank%d" % t) for t in range(PACK)]
+        a_bank = [psum.tile([P, H], F32, name="a_bank%d" % t, tag="bank%d" % (PACK + t)) for t in range(PACK)]
         for t in range(PACK):
             product(b_bank[t], xb, t, wbq, whole)
-        wa_grouped = [group_weight(wa_raw[0], "wa_grouped0", nc.scalar.copy), group_weight(wa_raw[1], "wa_grouped1", nc.vector.tensor_copy)]
-        a_bank = [psum.tile([P, H], F32, name="a_bank%d" % t, tag="bank%d" % (PACK + t)) for t in range(PACK)]
-        for h in range(2):
-            quantize(waq, halves[h], wa_grouped[h][:])
-            for t in range(PACK):
-                product(a_bank[t], xa, t, waq, halves[h])
+        for t in range(PACK):
+            product(a_bank[t], xa, t, waq, whole)
 
         ds = [tile([P, H], F32, "ds%d" % t) for t in range(PACK)]
         ga = [tile([P, W], F32, "ga%d" % t) for t in range(PACK)]
@@ -126,8 +140,8 @@ def tile_picked_momtputbnorm2_none_po_kernel(tc, x_words, x_scales, wa, wb, gt, 
             nc.vector.tensor_copy(ds[t][:], a_bank[t][:])
             nc.scalar.activation(ga[t][:], ds[t][:].indirect(n1_t[:]), ACT.Copy)
 
-        def fetch_b(t, copy, tag):
-            b_sb[t] = tile([P, H], F32, "b_sb%d" % t, tag)
+        def fetch_b(t, copy):
+            b_sb[t] = tile([P, H], F32, "b_sb%d" % t, at=2048 * t)
             copy(b_sb[t][:], b_bank[t][:])
             nc.scalar.activation(gb[t][:], b_sb[t][:].indirect(n2_t[:]), ACT.Copy)
 
@@ -143,19 +157,17 @@ def tile_picked_momtputbnorm2_none_po_kernel(tc, x_words, x_scales, wa, wb, gt, 
         def weigh_z2(t):
             nc.vector.tensor_scalar(out=z2_planes[:, t, :], in0=b_sb[t][:], scalar1=gi_t[:, t : t + 1], scalar2=None, op0=ALU.mult)
 
-        fetch_b(0, nc.scalar.copy, "wa_raw0")
-        fetch_b(1, nc.scalar.copy, "wa_grouped0")
+        fetch_b(0, nc.scalar.copy)
+        fetch_b(1, nc.scalar.copy)
+        fetch_b(2, nc.vector.tensor_copy)
         fetch_a(0)
         fetch_a(1)
-        fetch_b(2, nc.vector.tensor_copy, "wa_grouped1")
-        put(0)
+        fetch_b(3, nc.vector.tensor_copy)
         fetch_a(2)
-        fetch_b(3, nc.vector.tensor_copy, "ga0")
-        put(1)
         fetch_a(3)
-        put(2)
-        put(3)
-        z2_planes = tile([P, PACK, H], BF16, "z2_planes", "ga1")
+        for t in range(PACK):
+            put(t)
+        z2_planes = tile([P, PACK, H], BF16, "z2_planes", "ga0")
         z_planes = tile([P, PACK - 1, H], BF16, "z_planes")
         for t in range(PACK):
             weigh_z2(t)
@@ -201,37 +213,48 @@ def tile_picked_momtputbnorm2_none_po_kernel(tc, x_words, x_scales, wa, wb, gt, 
         out_rows = out_0.rearrange("(p u) n -> p u n", u=PACK)
         out_words = out_1[0].rearrange("p n r -> p (n r)").bitcast(I32)
         y_scales = tile([P, H], U8, "y_scales")
+        ident = tile([P, P], F32, "ident")
+        make_identity(nc, ident[:])
+        half = tile([P, 1], F32, "half")
+        nc.gpsimd.memset(half[:], 0.5)
         edges = [0, 256, 384, 512]
         chunks = range(len(edges) - 1)
         cols = [slice(edges[c], edges[c + 1]) for c in chunks]
         entries = [slice(edges[c] // 16, edges[c + 1] // 16) for c in chunks]
         width = [edges[c + 1] - edges[c] for c in chunks]
         y = [tile([P, PACK, width[c]], F32, "y%d" % c) for c in chunks]
-        far, den, root, top = {}, {}, {}, {}
+        far = [tile([P, PACK, 256], F32, "far0", at=8192), tile([P, PACK, P], F32, "far1", at=8192), tile([P, PACK, P], F32, "far2", at=10240)]
+        root = [tile([P, H], F32, "root0"), tile([P, H], F32, "root1"), tile([P, H], F32, "root2", at=12288), tile([P, H], F32, "root3")]
+        top = [tile([P, PACK, 256], F32, "top0"), tile([P, PACK, P], F32, "top1", at=10240), tile([P, PACK, P], F32, "top2", at=12288)]
+        inverse = [tile([P, H], F32, "inverse%d" % k) for k in range(PACK)]
+        place = [(0, 0), (0, P), (1, 0), (2, 0)]
+        den_bank, inv_bank = {}, {}
 
-        def fetch_far(c, us):
-            key = (c, us[0])
-            far[key] = tile([P, len(us), width[c]], F32, "far%d_%d" % key)
-            den[key] = tile([P, len(us), width[c]], F32, "den%d_%d" % key)
-            for i, u in enumerate(us):
-                nc.scalar.activation(far[key][:, i, :], size[u][:].indirect(n4_t[:, entries[c]]), ACT.Copy)
-                nc.vector.scalar_tensor_tensor(out=den[key][:, i, :], in0=size[u][:, cols[c]], scalar=0.5, in1=far[key][:, i, :], op0=ALU.add, op1=ALU.add)
+        def fetch_far(c, u):
+            nc.scalar.activation(far[c][:, u, :], size[u][:].indirect(n4_t[:, entries[c]]), ACT.Copy)
 
-        def invert(c, us):
-            key = (c, us[0])
-            root[key] = tile([P, len(us), width[c]], F32, "root%d_%d" % key)
-            nc.scalar.activation(root[key][:], den[key][:], ACT.Abs_reciprocal_sqrt)
-            nc.vector.tensor_tensor(out=far[key][:], in0=root[key][:], in1=root[key][:], op=ALU.mult)
+        def fetch_top(c, u):
+            nc.scalar.activation(top[c][:, u, :], cv[u][:].indirect(n3_t[:, entries[c]]), ACT.Copy)
 
-        def fetch_top(c, us, each):
-            key = (c, us[0])
-            top[key] = tile([P, len(us), width[c]], F32, "top%d_%d" % key, "den%d_%d" % key)
-            for i, u in enumerate(us):
-                nc.scalar.activation(top[key][:, i, :], cv[u][:].indirect(n3_t[:, entries[c]]), ACT.Copy)
-                if each:
-                    nc.vector.tensor_tensor(out=y[c][:, u, :], in0=top[key][:, i, :], in1=far[key][:, i, :], op=ALU.mult)
-            if not each:
-                nc.vector.tensor_tensor(out=y[c][:, us[0] : us[-1] + 1, :], in0=top[key][:], in1=far[key][:], op=ALU.mult)
+        def add_up(k, u):
+            c, first = place[k]
+            if u == 0:
+                den_bank[k] = psum.tile([P, PACK, P], F32, name="den_bank%d" % k, tag="bank%d" % (4 + k % 2))
+            nc.tensor.matmul(den_bank[k][:, u, :], lhsT=size[u][:, k * P : (k + 1) * P], rhs=ident[:], is_transpose=True, start=True, stop=False)
+            nc.tensor.matmul(den_bank[k][:, u, :], lhsT=far[c][:, u, first : first + P], rhs=ident[:], is_transpose=True, start=False, stop=True)
+
+        def take_root(k):
+            nc.scalar.activation(root[k][:], den_bank[k][:].rearrange("p u m -> p (u m)"), ACT.Abs_reciprocal_sqrt, bias=half[:])
+
+        def invert(k):
+            nc.vector.tensor_tensor(out=inverse[k][:], in0=root[k][:], in1=root[k][:], op=ALU.mult)
+            inv_bank[k] = psum.tile([P, PACK, P], F32, name="inv_bank%d" % k, tag="bank%d" % (6 + k % 2))
+            for u in range(PACK):
+                nc.tensor.transpose(inv_bank[k][:, u, :], inverse[k][:, u * P : (u + 1) * P], ident[:])
+
+        def divide(k, us=slice(0, PACK)):
+            c, first = place[k]
+            nc.vector.tensor_tensor(out=y[c][:, us, first : first + P], in0=inv_bank[k][:, us, :], in1=top[c][:, us, first : first + P], op=ALU.mult)
 
         def hand_out(c):
             nc.sync.dma_start(out_rows[:, :, cols[c]], y[c][:])
@@ -244,32 +267,43 @@ def tile_picked_momtputbnorm2_none_po_kernel(tc, x_words, x_scales, wa, wb, gt, 
 
         size_on_scalar(0)
         empty_cv(0)
-        fetch_far(0, [0])
-        empty_cv(1)
-        size_on_vector(1)
-        invert(0, [0])
-        fetch_top(0, [0], True)
-        fetch_far(0, [1])
+        fetch_far(0, 0)
+        size_on_scalar(1)
         empty_cv(2)
         size_on_vector(2)
-        invert(0, [1])
-        fetch_top(0, [1], True)
-        fetch_far(0, [2])
+        fetch_far(0, 1)
+        empty_cv(1)
+        fetch_top(0, 0)
+        fetch_top(0, 1)
         empty_cv(3)
         size_on_vector(3)
-        invert(0, [2])
-        fetch_top(0, [2], True)
-        fetch_far(0, [3])
-        invert(0, [3])
-        fetch_far(1, [0, 1, 2, 3])
-        fetch_top(0, [3], True)
-        fetch_far(2, [0, 1, 2, 3])
-        invert(1, [0, 1, 2, 3])
+        for u in (2, 3):
+            fetch_far(0, u)
+            fetch_top(0, u)
+        for u in range(PACK):
+            add_up(0, u)
+            add_up(1, u)
+        for k in range(2):
+            take_root(k)
+            invert(k)
+        for c in (1, 2):
+            for u in range(PACK):
+                fetch_far(c, u)
+                add_up(c + 1, u)
+        divide(0)
+        divide(1)
         hand_out(0)
-        fetch_top(1, [0, 1, 2, 3], False)
-        invert(2, [0, 1, 2, 3])
+        for k in (2, 3):
+            take_root(k)
+            invert(k)
+        for u in range(PACK):
+            fetch_top(1, u)
+        divide(2)
         hand_out(1)
-        fetch_top(2, [0, 1, 2, 3], True)
+        for u in range(PACK):
+            fetch_top(2, u)
+        divide(3, slice(0, 3))
+        divide(3, slice(3, 4))
         hand_out(2)
         for q in range(4):
             queue = nc.scalar if q % 2 else nc.sync

@@ -62,26 +62,35 @@ def tile_picked_momtputbnorm2_none_po_kernel(tc, x_words, x_scales, wa, wb, gt, 
         nc.vector.memset(xs[:].bitcast(I32), 0)
         for q in range(4):
             nc.scalar.dma_start(xs[32 * q : 32 * q + 4, :].bitcast(I32), x_scales[0, 4 * q : 4 * q + 4, :].bitcast(I32))
+        warm_in = tile([P, 1], F32, "warm_in")
+        nc.vector.memset(warm_in[:], 1.0)
+        warm_out = tile([P, 1], F32, "warm_out")
+        nc.scalar.activation(warm_out[:], warm_in[:], ACT.Abs_reciprocal_sqrt)
 
-        def load_weight_half(w, h, name, at=None):
-            raw = tile([P, PACK, HALF], F32, name, at=at)
-            nc.sync.dma_start(raw[:], w.rearrange("(p j) n -> p j n", j=PACK)[:, :, halves[h]])
+        def load_weight(w, part, name, at=None):
+            raw = tile([P, PACK, part.stop - part.start], F32, name, at=at)
+            nc.sync.dma_start(raw[:], w.rearrange("(p j) n -> p j n", j=PACK)[:, :, part])
             return raw
 
         two_t = load_list(two, "two_t")
         offs_t = load_list(offs, "offs_t")
-        wb_whole = tile([P, PACK, H], F32, "wb_whole")
-        nc.sync.dma_start(wb_whole[:], wb.rearrange("(p j) n -> p j n", j=PACK))
-        wa_raw = [load_weight_half(wa, 0, "wa_raw0")]
+        n2_t = load_list(n2, "n2_t")
+        wb_whole = load_weight(wb, whole, "wb_whole")
+        wa_parts = halves
+        wa_raw = [load_weight(wa, wa_parts[0], "wa_raw0")]
         xw = tile([P, T], I32, "xw")
         nc.sync.dma_start(xw[:], x_words[0].rearrange("p n r -> p (n r)").bitcast(I32))
-        wa_raw.append(load_weight_half(wa, 1, "wa_raw1", at=0))
-        n2_t = load_list(n2, "n2_t")
+        wa_raw.append(load_weight(wa, wa_parts[1], "wa_raw1", at=0))
         n1_t = load_list(n1, "n1_t")
-        gi_t = tile([P, PACK], F32, "gi_t")
-        nc.sync.dma_start(gi_t[:], gi.rearrange("(p t) o -> p (t o)", t=PACK))
-        gt_t = tile([P, PACK], F32, "gt_t")
-        nc.sync.dma_start(gt_t[:], gt.rearrange("(p t) o -> p (t o)", t=PACK))
+        ident = tile([P, P], F32, "ident")
+        make_identity(nc, ident[:])
+        half = tile([P, 1], F32, "half")
+        nc.gpsimd.memset(half[:], 0.5)
+        gate_rows = tile([P, P], F32, "gate_rows")
+        nc.gpsimd.memset(gate_rows[:], 0.0)
+        for first, gate in ((0, gi), (PACK, gt)):
+            nc.sync.dma_start(gate_rows[first : first + PACK, :].rearrange("t (q e) -> t q e", e=8),
+                              gate.rearrange("(q t e) o -> t q (e o)", t=PACK, e=8))
         n4_t = load_list(n4, "n4_t")
         n3_t = load_list(n3, "n3_t")
 
@@ -92,12 +101,13 @@ def tile_picked_momtputbnorm2_none_po_kernel(tc, x_words, x_scales, wa, wb, gt, 
 
         def deal_scales(picked, name):
             dealt = tile([P, S], U8, name + "_dealt")
-            nc.vector.tensor_copy(dealt[:].rearrange("p (t m) -> p m t", t=PACK), picked[:].rearrange("p (m t) -> p m t", t=PACK))
+            nc.vector.tensor_copy(dealt[:].bitcast(I32).rearrange("p (t q e) -> p t q e", t=PACK, e=2),
+                                  picked[:].bitcast(I32).rearrange("p (q t e) -> p t q e", t=PACK, e=2))
             return dealt
 
         def pick_words(lst, name):
             dealt = tile([P, S], U32, name)
-            nc.vector.tensor_copy(dealt[:].rearrange("p (t m) -> p m t", t=PACK), xw[:].bitcast(U32).indirect(lst[:]))
+            nc.vector.tensor_copy(dealt[:].rearrange("p (t q e) -> p q t e", t=PACK, e=8), xw[:].bitcast(U32).indirect(lst[:]))
             return dealt
 
         def group_weight(raw, name, copy):
@@ -112,8 +122,8 @@ def tile_picked_momtputbnorm2_none_po_kernel(tc, x_words, x_scales, wa, wb, gt, 
         wa_grouped = tile([P, H, PACK], BF16, "wa_grouped", at=4096)
         dst, src = interleave_views(wb_grouped[:], wb_whole[:])
         nc.scalar.copy(dst, src)
-        for h in range(2):
-            dst, src = interleave_views(wa_grouped[:, halves[h], :], wa_raw[h][:])
+        for part, raw in zip(wa_parts, wa_raw):
+            dst, src = interleave_views(wa_grouped[:, part, :], raw[:])
             nc.scalar.copy(dst, src)
         xb_picked = pick_scales(two_t, "xb_scales")
         xa_picked = pick_scales(offs_t, "xa_scales")
@@ -123,6 +133,11 @@ def tile_picked_momtputbnorm2_none_po_kernel(tc, x_words, x_scales, wa, wb, gt, 
         xb = (pick_words(two_t, "xb_words"), xb_scales)
         xa = (pick_words(offs_t, "xa_words"), xa_scales)
         quantize(waq, whole, wa_grouped[:])
+        gate_bank = psum.tile([P, P], F32, name="gate_bank", tag="bank7")
+        nc.tensor.transpose(gate_bank[:], gate_rows[:], ident[:])
+        gates = tile([P, 2 * PACK], F32, "gates")
+        nc.vector.tensor_copy(gates[:], gate_bank[:, 0 : 2 * PACK])
+        gi_t, gt_t = gates[:, 0:PACK], gates[:, PACK:]
         b_bank = [psum.tile([P, H], F32, name="b_bank%d" % t, tag="bank%d" % t) for t in range(PACK)]
         a_bank = [psum.tile([P, H], F32, name="a_bank%d" % t, tag="bank%d" % (PACK + t)) for t in range(PACK)]
         for t in range(PACK):
@@ -131,7 +146,7 @@ def tile_picked_momtputbnorm2_none_po_kernel(tc, x_words, x_scales, wa, wb, gt, 
             product(a_bank[t], xa, t, waq, whole)
 
         ds = [tile([P, H], F32, "ds%d" % t) for t in range(PACK)]
-        ga = [tile([P, W], F32, "ga%d" % t) for t in range(PACK)]
+        ga = [tile([P, W], F32, "ga%d" % t, at=16384 if t == 0 else None) for t in range(PACK)]
         gb = [tile([P, W], F32, "gb%d" % t) for t in range(PACK)]
         ra = [tile([P, W], F32, "ra%d" % t) for t in range(PACK)]
         b_sb = {}
@@ -149,9 +164,10 @@ def tile_picked_momtputbnorm2_none_po_kernel(tc, x_words, x_scales, wa, wb, gt, 
             nc.vector.scalar_tensor_tensor(out=ra[t][:], in0=ga[t][:], scalar=-0.5, in1=gb[t][:], op0=ALU.mult, op1=ALU.add)
             nc.scalar.activation(ds[t][:].indirect(n1_t[:]), ra[t][:], ACT.Copy)
 
-        def weigh_z(t):
-            nc.vector.tensor_scalar(out=z_planes[:, t, :].rearrange("p (u m) -> p m u", u=PACK),
-                                    in0=ds[t][:].rearrange("p (m u) -> p m u", u=PACK),
+        z_grouped = [tile([P, P, PACK], BF16, "z_grouped%d" % u, at=16384 + 1024 * u) for u in range(PACK)]
+
+        def weigh_z(t, u):
+            nc.vector.tensor_scalar(out=z_grouped[u][:, :, t], in0=ds[t][:].rearrange("p (m u) -> p u m", u=PACK)[:, u, :],
                                     scalar1=gt_t[:, t : t + 1], scalar2=None, op0=ALU.mult)
 
         def weigh_z2(t):
@@ -167,8 +183,7 @@ def tile_picked_momtputbnorm2_none_po_kernel(tc, x_words, x_scales, wa, wb, gt, 
         fetch_a(3)
         for t in range(PACK):
             put(t)
-        z2_planes = tile([P, PACK, H], BF16, "z2_planes", "ga0")
-        z_planes = tile([P, PACK - 1, H], BF16, "z_planes")
+        z2_planes = tile([P, PACK, H], BF16, "z2_planes", at=16384)
         for t in range(PACK):
             weigh_z2(t)
         z2_grouped = tile([P, H, PACK], BF16, "z2_grouped")
@@ -177,35 +192,35 @@ def tile_picked_momtputbnorm2_none_po_kernel(tc, x_words, x_scales, wa, wb, gt, 
         z2q = mx_tile("z2q", H)
         quantize(z2q, whole, z2_grouped[:])
         for t in range(PACK - 1):
-            weigh_z(t)
+            for u in range(PACK):
+                weigh_z(t, u)
 
         zq = mx_tile("zq", H)
-        z_grouped = [tile([P, P, PACK], BF16, "z_grouped%d" % u) for u in range(PACK)]
-        cv_bank = [psum.tile([P, H], F32, name="cv_bank%d" % u, tag="bank%d" % u) for u in range(PACK)]
+        cv_bank = {u: psum.tile([P, H], F32, name="cv_bank%d" % u, tag="bank%d" % u) for u in range(1, PACK)}
         cv = [tile([P, H], F32, "cv%d" % u) for u in range(PACK)]
         size = [tile([P, H], F32, "size%d" % u) for u in range(PACK)]
 
         last = PACK - 1
+        first_banks = [psum.tile([P, H], F32, name="cv_half%d" % h, tag="bank%d" % (4 * h)) for h in range(2)]
         for u in range(PACK):
-            dst, src = interleave_views(z_grouped[u][:, :, 0:last], z_planes[:, :, u * P : (u + 1) * P])
-            nc.vector.tensor_copy(dst, src)
-
-        def weigh_last(u):
-            nc.vector.tensor_scalar(out=z_grouped[u][:, :, last], in0=ds[last][:].rearrange("p (m u) -> p u m", u=PACK)[:, u, :],
-                                    scalar1=gt_t[:, last:], scalar2=None, op0=ALU.mult)
-
-        weigh_last(0)
-        for u in range(PACK):
-            if u + 1 < PACK:
-                weigh_last(u + 1)
+            weigh_z(last, u)
             quantize(zq, slice(u * P, (u + 1) * P), z_grouped[u][:])
-            product(cv_bank[u], zq, u, z2q, whole)
+            if u == 0:
+                for h in range(2):
+                    product(first_banks[h], zq, u, z2q, halves[h])
+            else:
+                product(cv_bank[u], zq, u, z2q, whole)
 
         def empty_cv(u):
             nc.vector.tensor_scalar(out=cv[u][:], in0=cv_bank[u][:], scalar1=0.0625, scalar2=None, op0=ALU.mult)
 
-        def size_on_scalar(u):
-            nc.scalar.activation(size[u][:], cv_bank[u][:], ACT.Abs, scale=0.0625)
+        def size_first():
+            for h in range(2):
+                nc.scalar.activation(size[0][:, halves[h]], first_banks[h][:, halves[h]], ACT.Abs, scale=0.0625)
+
+        def empty_first():
+            for h in range(2):
+                nc.vector.tensor_scalar(out=cv[0][:, halves[h]], in0=first_banks[h][:, halves[h]], scalar1=0.0625, scalar2=None, op0=ALU.mult)
 
         def size_on_vector(u):
             nc.vector.scalar_tensor_tensor(out=size[u][:], in0=cv_bank[u][:], scalar=-0.0625, in1=cv[u][:], op0=ALU.mult, op1=ALU.max)
@@ -213,10 +228,6 @@ def tile_picked_momtputbnorm2_none_po_kernel(tc, x_words, x_scales, wa, wb, gt, 
         out_rows = out_0.rearrange("(p u) n -> p u n", u=PACK)
         out_words = out_1[0].rearrange("p n r -> p (n r)").bitcast(I32)
         y_scales = tile([P, H], U8, "y_scales")
-        ident = tile([P, P], F32, "ident")
-        make_identity(nc, ident[:])
-        half = tile([P, 1], F32, "half")
-        nc.gpsimd.memset(half[:], 0.5)
         edges = [0, 256, 384, 512]
         chunks = range(len(edges) - 1)
         cols = [slice(edges[c], edges[c + 1]) for c in chunks]
@@ -256,33 +267,34 @@ def tile_picked_momtputbnorm2_none_po_kernel(tc, x_words, x_scales, wa, wb, gt, 
             c, first = place[k]
             nc.vector.tensor_tensor(out=y[c][:, us, first : first + P], in0=inv_bank[k][:, us, :], in1=top[c][:, us, first : first + P], op=ALU.mult)
 
-        def hand_out(c):
-            nc.sync.dma_start(out_rows[:, :, cols[c]], y[c][:])
-            y_grouped = tile([P, width[c], PACK], BF16, "y_grouped%d" % c)
-            dst, src = interleave_views(y_grouped[:], y[c][:])
-            nc.vector.tensor_copy(dst, src)
-            y_codes = tile([P, width[c]], U32, "y_codes%d" % c)
-            nc.vector.quantize_mx(out=y_codes[:].bitcast(FP8X4), scales=y_scales[:, cols[c]], in_=y_grouped[:].rearrange("p n j -> p (n j)"))
-            nc.sync.dma_start(out_words[:, cols[c]], y_codes[:].bitcast(I32))
+        y_grouped = [tile([P, HALF, PACK], BF16, "y_grouped%d" % h) for h in range(2)]
 
-        size_on_scalar(0)
-        empty_cv(0)
-        fetch_far(0, 0)
-        size_on_scalar(1)
-        empty_cv(2)
-        size_on_vector(2)
-        fetch_far(0, 1)
-        empty_cv(1)
-        fetch_top(0, 0)
-        fetch_top(0, 1)
-        empty_cv(3)
-        size_on_vector(3)
-        for u in (2, 3):
+        def store_and_round(c, copy):
+            nc.sync.dma_start(out_rows[:, :, cols[c]], y[c][:])
+            h, first = divmod(edges[c], HALF)
+            dst, src = interleave_views(y_grouped[h][:, first : first + width[c], :], y[c][:])
+            copy(dst, src)
+
+        def hand_on(h):
+            y_codes = tile([P, HALF], U32, "y_codes%d" % h)
+            nc.vector.quantize_mx(out=y_codes[:].bitcast(FP8X4), scales=y_scales[:, halves[h]], in_=y_grouped[h][:].rearrange("p n j -> p (n j)"))
+            nc.sync.dma_start(out_words[:, halves[h]], y_codes[:].bitcast(I32))
+
+        def fetch_first(u):
             fetch_far(0, u)
-            fetch_top(0, u)
-        for u in range(PACK):
             add_up(0, u)
             add_up(1, u)
+
+        size_first()
+        empty_cv(1)
+        empty_first()
+        size_on_vector(1)
+        for u in range(PACK):
+            if u > 1:
+                empty_cv(u)
+                size_on_vector(u)
+            fetch_first(u)
+            fetch_top(0, u)
         for k in range(2):
             take_root(k)
             invert(k)
@@ -292,19 +304,19 @@ def tile_picked_momtputbnorm2_none_po_kernel(tc, x_words, x_scales, wa, wb, gt, 
                 add_up(c + 1, u)
         divide(0)
         divide(1)
-        hand_out(0)
+        store_and_round(0, nc.vector.tensor_copy)
+        hand_on(0)
         for k in (2, 3):
             take_root(k)
             invert(k)
-        for u in range(PACK):
-            fetch_top(1, u)
-        divide(2)
-        hand_out(1)
-        for u in range(PACK):
-            fetch_top(2, u)
-        divide(3, slice(0, 3))
-        divide(3, slice(3, 4))
-        hand_out(2)
+        for c in (1, 2):
+            for first in (0, 2):
+                fetch_top(c, first)
+                fetch_top(c, first + 1)
+                divide(c + 1, slice(first, first + 2))
+        store_and_round(1, nc.scalar.copy)
+        store_and_round(2, nc.vector.tensor_copy)
+        hand_on(1)
         for q in range(4):
             queue = nc.scalar if q % 2 else nc.sync
             queue.dma_start(out_2[0, 4 * q : 4 * q + 4, :].bitcast(I32), y_scales[32 * q : 32 * q + 4, :].bitcast(I32))

from contextlib import ExitStack

import concourse.mybir as mybir
from concourse.masks import make_identity

F32 = mybir.dt.float32
BF16 = mybir.dt.bfloat16
I32 = mybir.dt.int32
U32 = mybir.dt.uint32
U16 = mybir.dt.uint16
U8 = mybir.dt.uint8
FP8X4 = mybir.dt.float8_e4m3fn_x4
ALU = mybir.AluOpType
ACT = mybir.ActivationFunctionType

P = 128
PACK = 4
K, T, S, H, W = 512, 2048, 512, 512, 256
HALF = 256
FLOPS = 3 * 2 * 512 * 512 * 512


def interleave_views(dst, src):
    return dst.rearrange("p (c i) j -> p c j i", i=4), src.rearrange("p j (c i) -> p c j i", i=4)


def tile_picked_momtputbnorm2_none_po_kernel(tc, x_words, x_scales, wa, wb, gt, gi, offs, two, n1, n2, n3, n4, out_0, out_1, out_2):
    nc = tc.nc
    with ExitStack() as ctx:
        lists = ctx.enter_context(tc.tile_pool(name="lists", bufs=1))
        sb = ctx.enter_context(tc.tile_pool(name="sb", bufs=1))
        shared = ctx.enter_context(tc.tile_pool(name="shared", bufs=1))
        psum = ctx.enter_context(tc.psum_pool(name="psum", bufs=1))

        def tile(shape, dtype, name, tag=None, at=None):
            if at is not None:
                return shared.tile(shape, dtype, name=name, align_bytes=64, offset=at)
            return sb.tile(shape, dtype, name=name, tag=tag or name, align_bytes=64)

        def load_list(src, name):
            held = lists.tile([P, src.shape[1]], U16, name=name)
            nc.sync.dma_start(held[:], src)
            return held

        def mx_tile(name, width):
            return tile([P, width], U32, name + "_codes"), tile([P, width], U8, name + "_scales")

        def quantize(operand, cols, grouped):
            codes, scales = operand
            nc.vector.quantize_mx(out=codes[:, cols].bitcast(FP8X4), scales=scales[:, cols],
                                  in_=grouped.rearrange("p n j -> p (n j)"))

        def product(bank, stationary, t, moving, cols):
            rows = slice(t * P, (t + 1) * P)
            nc.tensor.matmul_mx(out=bank[:, cols], lhsT=stationary[0][:, rows].bitcast(FP8X4), lhsT_scale=stationary[1][:, rows],
                                rhs=moving[0][:, cols].bitcast(FP8X4), rhs_scale=moving[1][:, cols], start=True, stop=True)

        halves = [slice(h * HALF, (h + 1) * HALF) for h in range(2)]
        whole = slice(0, H)

        xs = tile([P, T], U8, "xs")
        nc.vector.memset(xs[:].bitcast(I32), 0)
        for q in range(4):
            nc.scalar.dma_start(xs[32 * q : 32 * q + 4, :].bitcast(I32), x_scales[0, 4 * q : 4 * q + 4, :].bitcast(I32))
        warm_in = tile([P, 1], F32, "warm_in")
        nc.vector.memset(warm_in[:], 1.0)
        warm_out = tile([P, 1], F32, "warm_out")
        nc.scalar.activation(warm_out[:], warm_in[:], ACT.Abs_reciprocal_sqrt)

        def load_weight(w, part, name, at=None):
            raw = tile([P, PACK, part.stop - part.start], F32, name, at=at)
            nc.sync.dma_start(raw[:], w.rearrange("(p j) n -> p j n", j=PACK)[:, :, part])
            return raw

        two_t = load_list(two, "two_t")
        offs_t = load_list(offs, "offs_t")
        n2_t = load_list(n2, "n2_t")
        wb_whole = load_weight(wb, whole, "wb_whole")
        wa_parts = halves
        wa_raw = [load_weight(wa, wa_parts[0], "wa_raw0")]
        xw = tile([P, T], I32, "xw")
        nc.sync.dma_start(xw[:], x_words[0].rearrange("p n r -> p (n r)").bitcast(I32))
        wa_raw.append(load_weight(wa, wa_parts[1], "wa_raw1", at=0))
        n1_t = load_list(n1, "n1_t")
        ident = tile([P, P], F32, "ident")
        make_identity(nc, ident[:])
        half = tile([P, 1], F32, "half")
        nc.gpsimd.memset(half[:], 0.5)
        gate_rows = tile([P, P], F32, "gate_rows")
        nc.gpsimd.memset(gate_rows[:], 0.0)
        for first, gate in ((0, gi), (PACK, gt)):
            nc.sync.dma_start(gate_rows[first : first + PACK, :].rearrange("t (q e) -> t q e", e=8),
                              gate.rearrange("(q t e) o -> t q (e o)", t=PACK, e=8))
        n4_t = load_list(n4, "n4_t")
        n3_t = load_list(n3, "n3_t")

        def pick_scales(lst, name):
            picked = tile([P, S], U8, name + "_picked")
            nc.vector.tensor_copy(picked[:], xs[:].indirect(lst[:]))
            return picked

        def deal_scales(picked, name):
            dealt = tile([P, S], U8, name + "_dealt")
            nc.vector.tensor_copy(dealt[:].bitcast(I32).rearrange("p (t q e) -> p t q e", t=PACK, e=2),
                                  picked[:].bitcast(I32).rearrange("p (q t e) -> p t q e", t=PACK, e=2))
            return dealt

        def pick_words(lst, name):
            dealt = tile([P, S], U32, name)
            nc.vector.tensor_copy(dealt[:].rearrange("p (t q e) -> p q t e", t=PACK, e=8), xw[:].bitcast(U32).indirect(lst[:]))
            return dealt

        def group_weight(raw, name, copy):
            grouped = tile([P, HALF, PACK], BF16, name)
            dst, src = interleave_views(grouped[:], raw[:])
            copy(dst, src)
            return grouped

        wbq = mx_tile("wbq", H)
        waq = mx_tile("waq", H)
        wb_grouped = tile([P, H, PACK], BF16, "wb_grouped")
        wa_grouped = tile([P, H, PACK], BF16, "wa_grouped", at=4096)
        dst, src = interleave_views(wb_grouped[:], wb_whole[:])
        nc.scalar.copy(dst, src)
        for part, raw in zip(wa_parts, wa_raw):
            dst, src = interleave_views(wa_grouped[:, part, :], raw[:])
            nc.scalar.copy(dst, src)
        xb_picked = pick_scales(two_t, "xb_scales")
        xa_picked = pick_scales(offs_t, "xa_scales")
        xb_scales = deal_scales(xb_picked, "xb_scales")
        xa_scales = deal_scales(xa_picked, "xa_scales")
        quantize(wbq, whole, wb_grouped[:])
        xb = (pick_words(two_t, "xb_words"), xb_scales)
        xa = (pick_words(offs_t, "xa_words"), xa_scales)
        quantize(waq, whole, wa_grouped[:])
        gate_bank = psum.tile([P, P], F32, name="gate_bank", tag="bank7")
        nc.tensor.transpose(gate_bank[:], gate_rows[:], ident[:])
        gates = tile([P, 2 * PACK], F32, "gates")
        nc.vector.tensor_copy(gates[:], gate_bank[:, 0 : 2 * PACK])
        gi_t, gt_t = gates[:, 0:PACK], gates[:, PACK:]
        b_bank = [psum.tile([P, H], F32, name="b_bank%d" % t, tag="bank%d" % t) for t in range(PACK)]
        a_bank = [psum.tile([P, H], F32, name="a_bank%d" % t, tag="bank%d" % (PACK + t)) for t in range(PACK)]
        for t in range(PACK):
            product(b_bank[t], xb, t, wbq, whole)
        for t in range(PACK):
            product(a_bank[t], xa, t, waq, whole)

        ds = [tile([P, H], F32, "ds%d" % t) for t in range(PACK)]
        ga = [tile([P, W], F32, "ga%d" % t, at=16384 if t == 0 else None) for t in range(PACK)]
        gb = [tile([P, W], F32, "gb%d" % t) for t in range(PACK)]
        ra = [tile([P, W], F32, "ra%d" % t) for t in range(PACK)]
        b_sb = {}

        def fetch_a(t):
            nc.vector.tensor_copy(ds[t][:], a_bank[t][:])
            nc.scalar.activation(ga[t][:], ds[t][:].indirect(n1_t[:]), ACT.Copy)

        def fetch_b(t, copy):
            b_sb[t] = tile([P, H], F32, "b_sb%d" % t, at=2048 * t)
            copy(b_sb[t][:], b_bank[t][:])
            nc.scalar.activation(gb[t][:], b_sb[t][:].indirect(n2_t[:]), ACT.Copy)

        def put(t):
            nc.vector.scalar_tensor_tensor(out=ra[t][:], in0=ga[t][:], scalar=-0.5, in1=gb[t][:], op0=ALU.mult, op1=ALU.add)
            nc.scalar.activation(ds[t][:].indirect(n1_t[:]), ra[t][:], ACT.Copy)

        z_grouped = [tile([P, P, PACK], BF16, "z_grouped%d" % u, at=16384 + 1024 * u) for u in range(PACK)]

        def weigh_z(t, u):
            nc.vector.tensor_scalar(out=z_grouped[u][:, :, t], in0=ds[t][:].rearrange("p (m u) -> p u m", u=PACK)[:, u, :],
                                    scalar1=gt_t[:, t : t + 1], scalar2=None, op0=ALU.mult)

        def weigh_z2(t):
            nc.vector.tensor_scalar(out=z2_planes[:, t, :], in0=b_sb[t][:], scalar1=gi_t[:, t : t + 1], scalar2=None, op0=ALU.mult)

        fetch_b(0, nc.scalar.copy)
        fetch_b(1, nc.scalar.copy)
        fetch_b(2, nc.vector.tensor_copy)
        fetch_a(0)
        fetch_a(1)
        fetch_b(3, nc.vector.tensor_copy)
        fetch_a(2)
        fetch_a(3)
        for t in range(PACK):
            put(t)
        z2_planes = tile([P, PACK, H], BF16, "z2_planes", at=16384)
        for t in range(PACK):
            weigh_z2(t)
        z2_grouped = tile([P, H, PACK], BF16, "z2_grouped")
        dst, src = interleave_views(z2_grouped[:], z2_planes[:])
        nc.vector.tensor_copy(dst, src)
        z2q = mx_tile("z2q", H)
        quantize(z2q, whole, z2_grouped[:])
        for t in range(PACK - 1):
            for u in range(PACK):
                weigh_z(t, u)

        zq = mx_tile("zq", H)
        cv_bank = {u: psum.tile([P, H], F32, name="cv_bank%d" % u, tag="bank%d" % u) for u in range(1, PACK)}
        cv = [tile([P, H], F32, "cv%d" % u) for u in range(PACK)]
        size = [tile([P, H], F32, "size%d" % u) for u in range(PACK)]

        last = PACK - 1
        first_banks = [psum.tile([P, H], F32, name="cv_half%d" % h, tag="bank%d" % (4 * h)) for h in range(2)]
        for u in range(PACK):
            weigh_z(last, u)
            quantize(zq, slice(u * P, (u + 1) * P), z_grouped[u][:])
            if u == 0:
                for h in range(2):
                    product(first_banks[h], zq, u, z2q, halves[h])
            else:
                product(cv_bank[u], zq, u, z2q, whole)

        def empty_cv(u):
            nc.vector.tensor_scalar(out=cv[u][:], in0=cv_bank[u][:], scalar1=0.0625, scalar2=None, op0=ALU.mult)

        def size_first():
            for h in range(2):
                nc.scalar.activation(size[0][:, halves[h]], first_banks[h][:, halves[h]], ACT.Abs, scale=0.0625)

        def empty_first():
            for h in range(2):
                nc.vector.tensor_scalar(out=cv[0][:, halves[h]], in0=first_banks[h][:, halves[h]], scalar1=0.0625, scalar2=None, op0=ALU.mult)

        def size_on_vector(u):
            nc.vector.scalar_tensor_tensor(out=size[u][:], in0=cv_bank[u][:], scalar=-0.0625, in1=cv[u][:], op0=ALU.mult, op1=ALU.max)

        out_rows = out_0.rearrange("(p u) n -> p u n", u=PACK)
        out_words = out_1[0].rearrange("p n r -> p (n r)").bitcast(I32)
        y_scales = tile([P, H], U8, "y_scales")
        edges = [0, 256, 384, 512]
        chunks = range(len(edges) - 1)
        cols = [slice(edges[c], edges[c + 1]) for c in chunks]
        entries = [slice(edges[c] // 16, edges[c + 1] // 16) for c in chunks]
        width = [edges[c + 1] - edges[c] for c in chunks]
        y = [tile([P, PACK, width[c]], F32, "y%d" % c) for c in chunks]
        far = [tile([P, PACK, 256], F32, "far0", at=8192), tile([P, PACK, P], F32, "far1", at=8192), tile([P, PACK, P], F32, "far2", at=10240)]
        root = [tile([P, H], F32, "root0"), tile([P, H], F32, "root1"), tile([P, H], F32, "root2", at=12288), tile([P, H], F32, "root3")]
        top = [tile([P, PACK, 256], F32, "top0"), tile([P, PACK, P], F32, "top1", at=10240), tile([P, PACK, P], F32, "top2", at=12288)]
        inverse = [tile([P, H], F32, "inverse%d" % k) for k in range(PACK)]
        place = [(0, 0), (0, P), (1, 0), (2, 0)]
        den_bank, inv_bank = {}, {}

        def fetch_far(c, u):
            nc.scalar.activation(far[c][:, u, :], size[u][:].indirect(n4_t[:, entries[c]]), ACT.Copy)

        def fetch_top(c, u):
            nc.scalar.activation(top[c][:, u, :], cv[u][:].indirect(n3_t[:, entries[c]]), ACT.Copy)

        def add_up(k, u):
            c, first = place[k]
            if u == 0:
                den_bank[k] = psum.tile([P, PACK, P], F32, name="den_bank%d" % k, tag="bank%d" % (4 + k % 2))
            nc.tensor.matmul(den_bank[k][:, u, :], lhsT=size[u][:, k * P : (k + 1) * P], rhs=ident[:], is_transpose=True, start=True, stop=False)
            nc.tensor.matmul(den_bank[k][:, u, :], lhsT=far[c][:, u, first : first + P], rhs=ident[:], is_transpose=True, start=False, stop=True)

        def take_root(k):
            nc.scalar.activation(root[k][:], den_bank[k][:].rearrange("p u m -> p (u m)"), ACT.Abs_reciprocal_sqrt, bias=half[:])

        def invert(k):
            nc.vector.tensor_tensor(out=inverse[k][:], in0=root[k][:], in1=root[k][:], op=ALU.mult)
            inv_bank[k] = psum.tile([P, PACK, P], F32, name="inv_bank%d" % k, tag="bank%d" % (6 + k % 2))
            for u in range(PACK):
                nc.tensor.transpose(inv_bank[k][:, u, :], inverse[k][:, u * P : (u + 1) * P], ident[:])

        def divide(k, us=slice(0, PACK)):
            c, first = place[k]
            nc.vector.tensor_tensor(out=y[c][:, us, first : first + P], in0=inv_bank[k][:, us, :], in1=top[c][:, us, first : first + P], op=ALU.mult)

        y_grouped = [tile([P, HALF, PACK], BF16, "y_grouped%d" % h) for h in range(2)]

        def store_and_round(c, copy):
            nc.sync.dma_start(out_rows[:, :, cols[c]], y[c][:])
            h, first = divmod(edges[c], HALF)
            dst, src = interleave_views(y_grouped[h][:, first : first + width[c], :], y[c][:])
            copy(dst, src)

        def hand_on(h):
            y_codes = tile([P, HALF], U32, "y_codes%d" % h)
            nc.vector.quantize_mx(out=y_codes[:].bitcast(FP8X4), scales=y_scales[:, halves[h]], in_=y_grouped[h][:].rearrange("p n j -> p (n j)"))
            nc.sync.dma_start(out_words[:, halves[h]], y_codes[:].bitcast(I32))

        def fetch_first(u):
            fetch_far(0, u)
            add_up(0, u)
            add_up(1, u)

        size_first()
        empty_cv(1)
        empty_first()
        size_on_vector(1)
        for u in range(PACK):
            if u > 1:
                empty_cv(u)
                size_on_vector(u)
            fetch_first(u)
            fetch_top(0, u)
        for k in range(2):
            take_root(k)
            invert(k)
        for c in (1, 2):
            for u in range(PACK):
                fetch_far(c, u)
                add_up(c + 1, u)
        divide(0)
        divide(1)
        store_and_round(0, nc.vector.tensor_copy)
        hand_on(0)
        for k in (2, 3):
            take_root(k)
            invert(k)
        for c in (1, 2):
            for first in (0, 2):
                fetch_top(c, first)
                fetch_top(c, first + 1)
                divide(c + 1, slice(first, first + 2))
        store_and_round(1, nc.scalar.copy)
        store_and_round(2, nc.vector.tensor_copy)
        hand_on(1)
        for q in range(4):
            queue = nc.scalar if q % 2 else nc.sync
            queue.dma_start(out_2[0, 4 * q : 4 * q + 4, :].bitcast(I32), y_scales[32 * q : 32 * q + 4, :].bitcast(I32))
